import numpy as np
import ml_dtypes

BF16 = ml_dtypes.bfloat16


def bf(x):
    return np.asarray(x, np.float32).astype(BF16)


def f32(x):
    return np.asarray(x, np.float32)


def f64(x):
    return np.asarray(x).astype(np.float64)


def striped(idx):
    return np.tile(idx.reshape(-1, 16).T, (8, 1))


S, K, M, N, E, Q = 512, 128, 256, 384, 4, 96


def setup_inputs():
    return {"base": bf(np.random.standard_normal((M, S))), "x": bf(np.random.standard_normal((K, N))), "w": bf(np.random.standard_normal((E, K, M)) / np.sqrt(K)), "c": f32(0.2 + 0.8 * np.random.random_sample((1, S))), "offs": striped(np.random.permutation(S)[:N])}


def reference(base, x, w, c, offs):
    idx = offs[:16].T.reshape(-1)
    z = f64(base).copy()
    for e in range(E):
        z[:, idx[e * Q : (e + 1) * Q]] += f64(w)[e].T @ f64(x)[:, e * Q : (e + 1) * Q]
    return z * f64(c)

@@ -1,0 +1,58 @@
+import concourse.mybir as mybir
+from concourse.masks import make_identity
+
+BF16, F32, U16 = mybir.dt.bfloat16, mybir.dt.float32, mybir.dt.uint16
+
+P = 128
+TOKENS = 512
+FEATURES = 256
+BLOCKS = FEATURES // P
+EXPERTS = 4
+PIECE = 96
+ENTRIES = EXPERTS * PIECE
+PIECE_COLUMNS = PIECE // 16
+
+FLOPS = 2 * P * FEATURES * ENTRIES
+
+
+def tile_scatter_matmul_kernel(tc, base, x, w, c, offs, out):
+    nc = tc.nc
+    with (
+        tc.tile_pool(name="held", bufs=1) as held,
+        tc.psum_pool(name="banks", bufs=1) as banks,
+    ):
+        offsets = held.tile([P, ENTRIES // 16], U16, name="offsets")
+        nc.sync.dma_start(offsets[:], offs)
+
+        base_sb = held.tile([P, BLOCKS, TOKENS], BF16, name="base_sb")
+        nc.scalar.dma_start(base_sb[:], base.rearrange("(b p) t -> p b t", p=P))
+
+        x_sb = held.tile([P, ENTRIES], BF16, name="x_sb")
+        nc.sync.dma_start(x_sb[:], x)
+
+        w_sb = held.tile([P, EXPERTS, FEATURES], BF16, name="w_sb")
+        nc.sync.dma_start(w_sb[:], w.rearrange("e k m -> k e m"))
+
+        c_sb = held.tile([P, TOKENS], F32, name="c_sb")
+        nc.scalar.dma_start(c_sb[:], c.partition_broadcast(P))
+
+        identity = held.tile([P, P], BF16, name="identity")
+        make_identity(nc, identity[:])
+
+        windows = [banks.tile([P, TOKENS], F32, name=f"window{b}") for b in range(BLOCKS)]
+        for b in range(BLOCKS):
+            nc.tensor.matmul(windows[b][:], identity[:], base_sb[:, b, :], start=True, stop=False)
+
+        for b in range(BLOCKS):
+            for e in range(EXPERTS):
+                nc.tensor.matmul(
+                    windows[b][:].indirect(offsets[:, e * PIECE_COLUMNS : (e + 1) * PIECE_COLUMNS]),
+                    w_sb[:, e, b * P : (b + 1) * P],
+                    x_sb[:, e * PIECE : (e + 1) * PIECE],
+                    start=False,
+                    stop=(e == EXPERTS - 1),
+                )
+
+            scaled = held.tile([P, TOKENS], F32, name=f"scaled{b}")
+            nc.vector.tensor_tensor(scaled[:], windows[b][:], c_sb[:], mybir.AluOpType.mult)
+            nc.sync.dma_start(out[b * P : (b + 1) * P, :], scaled[:])

@@ -21,33 +21,38 @@ def tile_scatter_matmul_kernel(tc, base, x, w, c, offs, out):
         tc.tile_pool(name="held", bufs=1) as held,
         tc.psum_pool(name="banks", bufs=1) as banks,
     ):
+        zeros = held.tile([P, TOKENS], BF16, name="zeros")
+        nc.gpsimd.memset(zeros[:].bitcast(F32), 0.0)
+        unread = banks.tile([P, TOKENS], F32, name="unread")
+        for i in range(4):
+            nc.tensor.matmul(unread[:], zeros[:, 0:P], zeros[:], start=True, stop=True)
+
         offsets = held.tile([P, ENTRIES // 16], U16, name="offsets")
-        nc.sync.dma_start(offsets[:], offs)
-
-        base_sb = held.tile([P, BLOCKS, TOKENS], BF16, name="base_sb")
-        nc.scalar.dma_start(base_sb[:], base.rearrange("(b p) t -> p b t", p=P))
-
+        base_sb = [held.tile([P, TOKENS], BF16, name=f"base_sb{b}") for b in range(BLOCKS)]
         x_sb = held.tile([P, ENTRIES], BF16, name="x_sb")
-        nc.sync.dma_start(x_sb[:], x)
-
-        w_sb = held.tile([P, EXPERTS, FEATURES], BF16, name="w_sb")
-        nc.sync.dma_start(w_sb[:], w.rearrange("e k m -> k e m"))
-
+        w_sb = [held.tile([P, EXPERTS // 2, FEATURES], BF16, name=f"w_sb{h}") for h in range(2)]
         c_sb = held.tile([P, TOKENS], F32, name="c_sb")
-        nc.scalar.dma_start(c_sb[:], c.partition_broadcast(P))
+
+        nc.sync.dma_start(offsets[:], offs)
+        nc.sync.dma_start(base_sb[0][:], base[0:P, :])
+        nc.scalar.dma_start(base_sb[1][:], base[P : 2 * P, :])
+        nc.scalar.dma_start(x_sb[:], x)
+        nc.sync.dma_start(w_sb[0][:], w[0 : EXPERTS // 2].rearrange("e k m -> k e m"))
+        nc.scalar.dma_start(w_sb[1][:], w[EXPERTS // 2 : EXPERTS].rearrange("e k m -> k e m"))
+        nc.sync.dma_start(c_sb[:], c.partition_broadcast(P))
 
         identity = held.tile([P, P], BF16, name="identity")
         make_identity(nc, identity[:])
 
         windows = [banks.tile([P, TOKENS], F32, name=f"window{b}") for b in range(BLOCKS)]
         for b in range(BLOCKS):
-            nc.tensor.matmul(windows[b][:], identity[:], base_sb[:, b, :], start=True, stop=False)
+            nc.tensor.matmul(windows[b][:], identity[:], base_sb[b][:], start=True, stop=False)
 
         for b in range(BLOCKS):
             for e in range(EXPERTS):
                 nc.tensor.matmul(
                     windows[b][:].indirect(offsets[:, e * PIECE_COLUMNS : (e + 1) * PIECE_COLUMNS]),
-                    w_sb[:, e, b * P : (b + 1) * P],
+                    w_sb[e // 2][:, e % 2, b * P : (b + 1) * P],
                     x_sb[:, e * PIECE : (e + 1) * PIECE],
                     start=False,
                     stop=(e == EXPERTS - 1),

@@ -7,6 +7,7 @@ P = 128
 TOKENS = 512
 FEATURES = 256
 BLOCKS = FEATURES // P
+HALF = TOKENS // 2
 EXPERTS = 4
 PIECE = 96
 ENTRIES = EXPERTS * PIECE
@@ -33,8 +34,8 @@ def tile_scatter_matmul_kernel(tc, base, x, w, c, offs, out):
         w_sb = [held.tile([P, EXPERTS // 2, FEATURES], BF16, name=f"w_sb{h}") for h in range(2)]
         c_sb = held.tile([P, TOKENS], F32, name="c_sb")
 
-        nc.sync.dma_start(offsets[:], offs)
         nc.sync.dma_start(base_sb[0][:], base[0:P, :])
+        nc.sync.dma_start(offsets[:], offs)
         nc.scalar.dma_start(base_sb[1][:], base[P : 2 * P, :])
         nc.scalar.dma_start(x_sb[:], x)
         nc.sync.dma_start(w_sb[0][:], w[0 : EXPERTS // 2].rearrange("e k m -> k e m"))
@@ -59,5 +60,9 @@ def tile_scatter_matmul_kernel(tc, base, x, w, c, offs, out):
                 )
 
             scaled = held.tile([P, TOKENS], F32, name=f"scaled{b}")
-            nc.vector.tensor_tensor(scaled[:], windows[b][:], c_sb[:], mybir.AluOpType.mult)
-            nc.sync.dma_start(out[b * P : (b + 1) * P, :], scaled[:])
+            for half, queue in enumerate((nc.sync, nc.scalar)):
+                columns = slice(half * HALF, (half + 1) * HALF)
+                nc.vector.tensor_tensor(
+                    scaled[:, columns], windows[b][:, columns], c_sb[:, columns], mybir.AluOpType.mult
+                )
+                queue.dma_start(out[b * P : (b + 1) * P, columns], scaled[:, columns])

@@ -32,15 +32,22 @@ def tile_scatter_matmul_kernel(tc, base, x, w, c, offs, out):
         base_sb = [held.tile([P, TOKENS], BF16, name=f"base_sb{b}") for b in range(BLOCKS)]
         x_sb = held.tile([P, ENTRIES], BF16, name="x_sb")
         w_sb = [held.tile([P, EXPERTS // 2, FEATURES], BF16, name=f"w_sb{h}") for h in range(2)]
-        c_sb = held.tile([P, TOKENS], F32, name="c_sb")
+        c_row = held.tile([1, TOKENS], F32, name="c_row")
 
+        nc.scalar.dma_start(c_row[:], c)
         nc.sync.dma_start(base_sb[0][:], base[0:P, :])
         nc.sync.dma_start(offsets[:], offs)
         nc.scalar.dma_start(base_sb[1][:], base[P : 2 * P, :])
         nc.scalar.dma_start(x_sb[:], x)
         nc.sync.dma_start(w_sb[0][:], w[0 : EXPERTS // 2].rearrange("e k m -> k e m"))
         nc.scalar.dma_start(w_sb[1][:], w[EXPERTS // 2 : EXPERTS].rearrange("e k m -> k e m"))
-        nc.sync.dma_start(c_sb[:], c.partition_broadcast(P))
+
+        ones_row = held.tile([1, P], F32, name="ones_row")
+        nc.vector.memset(ones_row[:], 1.0)
+        c_bank = banks.tile([P, TOKENS], F32, name="c_bank")
+        nc.tensor.matmul(c_bank[:], ones_row[:], c_row[:], start=True, stop=True)
+        c_sb = held.tile([P, TOKENS], F32, name="c_sb")
+        nc.vector.tensor_copy(c_sb[:], c_bank[:])
 
         identity = held.tile([P, P], BF16, name="identity")
         make_identity(nc, identity[:])

@@ -32,9 +32,9 @@ def tile_scatter_matmul_kernel(tc, base, x, w, c, offs, out):
         base_sb = [held.tile([P, TOKENS], BF16, name=f"base_sb{b}") for b in range(BLOCKS)]
         x_sb = held.tile([P, ENTRIES], BF16, name="x_sb")
         w_sb = [held.tile([P, EXPERTS // 2, FEATURES], BF16, name=f"w_sb{h}") for h in range(2)]
-        c_row = held.tile([1, TOKENS], F32, name="c_row")
+        c_col = held.tile([P, TOKENS // P], F32, name="c_col")
 
-        nc.scalar.dma_start(c_row[:], c)
+        nc.scalar.dma_start(c_col[:], c.rearrange("o (p j) -> p (o j)", p=P))
         nc.sync.dma_start(base_sb[0][:], base[0:P, :])
         nc.sync.dma_start(offsets[:], offs)
         nc.scalar.dma_start(base_sb[1][:], base[P : 2 * P, :])
@@ -42,15 +42,16 @@ def tile_scatter_matmul_kernel(tc, base, x, w, c, offs, out):
         nc.sync.dma_start(w_sb[0][:], w[0 : EXPERTS // 2].rearrange("e k m -> k e m"))
         nc.scalar.dma_start(w_sb[1][:], w[EXPERTS // 2 : EXPERTS].rearrange("e k m -> k e m"))
 
-        ones_row = held.tile([1, P], F32, name="ones_row")
-        nc.vector.memset(ones_row[:], 1.0)
-        c_bank = banks.tile([P, TOKENS], F32, name="c_bank")
-        nc.tensor.matmul(c_bank[:], ones_row[:], c_row[:], start=True, stop=True)
-        c_sb = held.tile([P, TOKENS], F32, name="c_sb")
-        nc.vector.tensor_copy(c_sb[:], c_bank[:])
-
+        identity_f32 = held.tile([P, P], F32, name="identity_f32")
+        make_identity(nc, identity_f32[:])
         identity = held.tile([P, P], BF16, name="identity")
         make_identity(nc, identity[:])
+
+        c_bank = banks.tile([P, TOKENS // P, P], F32, name="c_bank")
+        for j in range(TOKENS // P):
+            nc.tensor.transpose(c_bank[:, j, :], c_col[:, j : j + 1].to_broadcast([P, P]), identity_f32[:])
+        c_sb = held.tile([P, TOKENS], F32, name="c_sb")
+        nc.vector.tensor_copy(c_sb[:].rearrange("p (n j) -> p n j", j=TOKENS // P), c_bank[:].rearrange("p j n -> p n j"))
 
         windows = [banks.tile([P, TOKENS], F32, name=f"window{b}") for b in range(BLOCKS)]
         for b in range(BLOCKS):

@@ -31,7 +31,7 @@ def tile_scatter_matmul_kernel(tc, base, x, w, c, offs, out):
         offsets = held.tile([P, ENTRIES // 16], U16, name="offsets")
         base_sb = [held.tile([P, TOKENS], BF16, name=f"base_sb{b}") for b in range(BLOCKS)]
         x_sb = held.tile([P, ENTRIES], BF16, name="x_sb")
-        w_sb = [held.tile([P, EXPERTS // 2, FEATURES], BF16, name=f"w_sb{h}") for h in range(2)]
+        w_sb = [held.tile([P, FEATURES], BF16, name=f"w_sb{e}") for e in range(EXPERTS)]
         c_col = held.tile([P, TOKENS // P], F32, name="c_col")
 
         nc.scalar.dma_start(c_col[:], c.rearrange("o (p j) -> p (o j)", p=P))
@@ -39,8 +39,9 @@ def tile_scatter_matmul_kernel(tc, base, x, w, c, offs, out):
         nc.sync.dma_start(offsets[:], offs)
         nc.scalar.dma_start(base_sb[1][:], base[P : 2 * P, :])
         nc.scalar.dma_start(x_sb[:], x)
-        nc.sync.dma_start(w_sb[0][:], w[0 : EXPERTS // 2].rearrange("e k m -> k e m"))
-        nc.scalar.dma_start(w_sb[1][:], w[EXPERTS // 2 : EXPERTS].rearrange("e k m -> k e m"))
+        for e in range(EXPERTS):
+            queue = (nc.sync, nc.scalar)[e % 2]
+            queue.dma_start(w_sb[e][:], w[e])
 
         identity_f32 = held.tile([P, P], F32, name="identity_f32")
         make_identity(nc, identity_f32[:])
@@ -61,7 +62,7 @@ def tile_scatter_matmul_kernel(tc, base, x, w, c, offs, out):
             for e in range(EXPERTS):
                 nc.tensor.matmul(
                     windows[b][:].indirect(offsets[:, e * PIECE_COLUMNS : (e + 1) * PIECE_COLUMNS]),
-                    w_sb[e // 2][:, e % 2, b * P : (b + 1) * P],
+                    w_sb[e][:, b * P : (b + 1) * P],
                     x_sb[:, e * PIECE : (e + 1) * PIECE],
                     start=False,
                     stop=(e == EXPERTS - 1),

@@ -46,7 +46,7 @@ def tile_scatter_matmul_kernel(tc, base, x, w, c, offs, out):
         identity_f32 = held.tile([P, P], F32, name="identity_f32")
         make_identity(nc, identity_f32[:])
         identity = held.tile([P, P], BF16, name="identity")
-        make_identity(nc, identity[:])
+        nc.vector.tensor_copy(identity[:], identity_f32[:])
 
         c_bank = banks.tile([P, TOKENS // P, P], F32, name="c_bank")
         for j in range(TOKENS // P):

@@ -69,9 +69,9 @@ def tile_scatter_matmul_kernel(tc, base, x, w, c, offs, out):
                 )
 
             scaled = held.tile([P, TOKENS], F32, name=f"scaled{b}")
-            for half, queue in enumerate((nc.sync, nc.scalar)):
+            for half in range(2):
                 columns = slice(half * HALF, (half + 1) * HALF)
                 nc.vector.tensor_tensor(
                     scaled[:, columns], windows[b][:, columns], c_sb[:, columns], mybir.AluOpType.mult
                 )
-                queue.dma_start(out[b * P : (b + 1) * P, columns], scaled[:, columns])
+                nc.scalar.dma_start(out[b * P : (b + 1) * P, columns], scaled[:, columns])

@@ -22,11 +22,13 @@ def tile_scatter_matmul_kernel(tc, base, x, w, c, offs, out):
         tc.tile_pool(name="held", bufs=1) as held,
         tc.psum_pool(name="banks", bufs=1) as banks,
     ):
-        zeros = held.tile([P, TOKENS], BF16, name="zeros")
+        zeros = held.tile([P, P], BF16, name="zeros")
         nc.gpsimd.memset(zeros[:].bitcast(F32), 0.0)
-        unread = banks.tile([P, TOKENS], F32, name="unread")
+        unread = banks.tile([P, TOKENS // P, P], F32, name="unread")
         for i in range(4):
-            nc.tensor.matmul(unread[:], zeros[:, 0:P], zeros[:], start=True, stop=True)
+            nc.tensor.matmul(
+                unread[:], zeros[:], zeros[:].unsqueeze(1).to_broadcast([P, TOKENS // P, P]), start=True, stop=True
+            )
 
         offsets = held.tile([P, ENTRIES // 16], U16, name="offsets")
         base_sb = [held.tile([P, TOKENS], BF16, name=f"base_sb{b}") for b in range(BLOCKS)]
@@ -35,8 +37,8 @@ def tile_scatter_matmul_kernel(tc, base, x, w, c, offs, out):
         c_col = held.tile([P, TOKENS // P], F32, name="c_col")
 
         nc.scalar.dma_start(c_col[:], c.rearrange("o (p j) -> p (o j)", p=P))
-        nc.sync.dma_start(base_sb[0][:], base[0:P, :])
         nc.sync.dma_start(offsets[:], offs)
+        nc.sync.dma_start(base_sb[0][:], base[0:P, :])
         nc.scalar.dma_start(base_sb[1][:], base[P : 2 * P, :])
         nc.scalar.dma_start(x_sb[:], x)
         for e in range(EXPERTS):

import concourse.mybir as mybir
from concourse.masks import make_identity

BF16, F32, U16 = mybir.dt.bfloat16, mybir.dt.float32, mybir.dt.uint16

P = 128
TOKENS = 512
FEATURES = 256
BLOCKS = FEATURES // P
HALF = TOKENS // 2
EXPERTS = 4
PIECE = 96
ENTRIES = EXPERTS * PIECE
PIECE_COLUMNS = PIECE // 16

FLOPS = 2 * P * FEATURES * ENTRIES


def tile_scatter_matmul_kernel(tc, base, x, w, c, offs, out):
    nc = tc.nc
    with (
        tc.tile_pool(name="held", bufs=1) as held,
        tc.psum_pool(name="banks", bufs=1) as banks,
    ):
        zeros = held.tile([P, P], BF16, name="zeros")
        nc.gpsimd.memset(zeros[:].bitcast(F32), 0.0)
        unread = banks.tile([P, TOKENS // P, P], F32, name="unread")
        for i in range(4):
            nc.tensor.matmul(
                unread[:], zeros[:], zeros[:].unsqueeze(1).to_broadcast([P, TOKENS // P, P]), start=True, stop=True
            )

        offsets = held.tile([P, ENTRIES // 16], U16, name="offsets")
        base_sb = [held.tile([P, TOKENS], BF16, name=f"base_sb{b}") for b in range(BLOCKS)]
        x_sb = held.tile([P, ENTRIES], BF16, name="x_sb")
        w_sb = [held.tile([P, FEATURES], BF16, name=f"w_sb{e}") for e in range(EXPERTS)]
        c_col = held.tile([P, TOKENS // P], F32, name="c_col")

        nc.scalar.dma_start(c_col[:], c.rearrange("o (p j) -> p (o j)", p=P))
        nc.sync.dma_start(offsets[:], offs)
        nc.sync.dma_start(base_sb[0][:], base[0:P, :])
        nc.scalar.dma_start(base_sb[1][:], base[P : 2 * P, :])
        nc.scalar.dma_start(x_sb[:], x)
        for e in range(EXPERTS):
            queue = (nc.sync, nc.scalar)[e % 2]
            queue.dma_start(w_sb[e][:], w[e])

        identity_f32 = held.tile([P, P], F32, name="identity_f32")
        make_identity(nc, identity_f32[:])
        identity = held.tile([P, P], BF16, name="identity")
        nc.vector.tensor_copy(identity[:], identity_f32[:])

        c_bank = banks.tile([P, TOKENS // P, P], F32, name="c_bank")
        for j in range(TOKENS // P):
            nc.tensor.transpose(c_bank[:, j, :], c_col[:, j : j + 1].to_broadcast([P, P]), identity_f32[:])
        c_sb = held.tile([P, TOKENS], F32, name="c_sb")
        nc.vector.tensor_copy(c_sb[:].rearrange("p (n j) -> p n j", j=TOKENS // P), c_bank[:].rearrange("p j n -> p n j"))

        windows = [banks.tile([P, TOKENS], F32, name=f"window{b}") for b in range(BLOCKS)]
        for b in range(BLOCKS):
            nc.tensor.matmul(windows[b][:], identity[:], base_sb[b][:], start=True, stop=False)

        for b in range(BLOCKS):
            for e in range(EXPERTS):
                nc.tensor.matmul(
                    windows[b][:].indirect(offsets[:, e * PIECE_COLUMNS : (e + 1) * PIECE_COLUMNS]),
                    w_sb[e][:, b * P : (b + 1) * P],
                    x_sb[:, e * PIECE : (e + 1) * PIECE],
                    start=False,
                    stop=(e == EXPERTS - 1),
                )

            scaled = held.tile([P, TOKENS], F32, name=f"scaled{b}")
            for half in range(2):
                columns = slice(half * HALF, (half + 1) * HALF)
                nc.vector.tensor_tensor(
                    scaled[:, columns], windows[b][:, columns], c_sb[:, columns], mybir.AluOpType.mult
                )
                nc.scalar.dma_start(out[b * P : (b + 1) * P, columns], scaled[:, columns])
